import numpy as np
import ml_dtypes


def mxq(x, axis, fmt="e4m3"):
    dtype, down = {"e4m3": (ml_dtypes.float8_e4m3fn, 7), "e5m2": (ml_dtypes.float8_e5m2, 14)}[fmt]
    v = np.moveaxis(np.asarray(x, np.float32).astype(ml_dtypes.bfloat16).astype(np.float64), axis, -1)
    blocks = v.reshape(v.shape[:-1] + (-1, 32))
    amax = np.abs(blocks).max(-1, keepdims=True)
    byte = np.maximum(np.where(amax > 0, np.frexp(amax)[1] - 1 + 127, 0) - down, 1)
    scale = np.exp2(byte - 127.0)
    codes = (blocks / scale).astype(np.float32).astype(dtype).astype(np.float64)
    return np.moveaxis((codes * scale).reshape(v.shape), -1, axis)


WIDE = False


def mx_kscale(k, group=512):
    if not WIDE:
        return np.ones(k)
    levels = np.array([10, -10, 5, -5, 0])
    if group != 512:
        return np.exp2(np.random.permutation(np.resize(levels, k // group))).repeat(group)
    if k % 512:
        return np.exp2(np.random.permutation(np.resize(levels, k // 32))).repeat(32)
    a = np.empty((k // 512, 16))
    for p in range(k // 512):
        a[p, :8] = np.random.permutation(np.resize(levels, 8))
        for g in range(8):
            far = levels[np.abs(levels - a[p, g]) >= 10]
            a[p, g + 8] = far[np.random.randint(len(far))]
    return np.exp2(a.ravel()).repeat(32)


def f64(x):
    return np.asarray(x).astype(np.float64)


H, D, N = 4, 256, 512


def setup_inputs():
    n = np.random.standard_normal
    s = mx_kscale(D, 0)[:, None]
    S = n((H, D, 128))
    S[:, :, 127] = np.random.uniform(0.5, 1.5, (H, D))
    return {
        "q": n((H, D, N)).astype(np.float32),
        "qa": (np.random.uniform(0.5, 2.0, (D, 1)) * s).astype(np.float32),
        "S": (S / s).astype(np.float32),
    }


def reference(q, qa, S):
    fq = (np.square(f64(q)) + 0.125) * f64(qa)
    y = mxq(fq, 1, "e4m3").transpose(0, 2, 1) @ mxq(f64(S), 1, "e4m3")
    y = y / y[:, :, 127:128]
    return y

@@ -1,0 +1,189 @@
+from contextlib import ExitStack
+
+import concourse.mybir as mybir
+
+F32 = mybir.dt.float32
+BF16 = mybir.dt.bfloat16
+U32 = mybir.dt.uint32
+U8 = mybir.dt.uint8
+FP8X4 = mybir.dt.float8_e4m3fn_x4
+ACT = mybir.ActivationFunctionType
+ALU = mybir.AluOpType
+
+H, D, N, E = 4, 256, 512, 128
+P = 128
+FLOPS = 2 * H * D * N * E
+
+GROUPS = [(0,0,2),(0,256,2),(1,0,2),(1,256,1),(1,384,1)]
+PIECES = [(0,0,64),(0,64,64),(1,0,64),(1,64,64),(2,0,64),(2,64,64),(3,0,128),(4,0,128)]
+LOADS = [(0,0,128),(0,128,128),(0,256,128),(0,384,128),(1,0,128),(1,128,128),(1,256,128),(1,384,128)]
+SYNC = "lq:y0 w:a warm:0 lq:y1 lq:y2 lq:y3 ls:y0 lq:y4 lq:y5 lq:y6 ls:y1 lq:y7"
+ORDER = "wide:0 sq:0 sq:1 W:0 W:1 sq:2 sq:3 W:2 scs:0 Q:0 W:3 sQ:0 Q:1 sq:4 M:0 W:4 R:00 sq:5 W:5 sq:6 R:01 M:1 scs:1 W:6 sQ:1 R:10 Q:3 R:11 sq:7 Q:2 M:3 W:7 es:00 R:30 M:2 es:01 ev:10 es:11 Q:4 R:31 R:21 es:30 es:31 R:20 M:4 st:y0 st:y1 ev:20 R:40 es:21 st:y3 es:40 R:41 st:y2 es:41 st:y4"
+
+
+def tile_rows_read_sq_norm_kernel(tc, q, qa, S, out):
+    nc = tc.nc
+    q_rows = q.rearrange("h (p j) n -> (h p) j n", j=4)
+    s_rows = S.rearrange("h (p j) e -> (h p) j e", j=4)
+    qa_rows = qa.rearrange("(p j) o -> p (j o)", j=4)
+
+    with ExitStack() as ctx:
+        sb = ctx.enter_context(tc.tile_pool(name="sb", bufs=1))
+        ps = ctx.enter_context(tc.psum_pool(name="ps", bufs=1))
+        ctx.enter_context(tc.manual_schedule())
+
+        weight = sb.tile([P, 4], F32, name="weight")
+        wide = sb.tile([P, 4 * max(mc for g, m0, mc in PIECES)], F32, name="wide", align_bytes=64)
+        warm = sb.tile([P, 1], F32, name="warm")
+        warm_out = sb.tile([P, 1], F32, name="warm_out")
+        raw = [sb.tile([P, 4, w], F32, name="raw%d" % i, align_bytes=64) for i, (s, n0, w) in enumerate(LOADS)]
+        s_raw = [sb.tile([P, 4, E], F32, name="s_raw%d" % s, align_bytes=64) for s in range(2)]
+        s_bf = [sb.tile([P, E, 4], BF16, name="s_bf%d" % s, align_bytes=64) for s in range(2)]
+        s_codes = [sb.tile([P, E], U32, name="s_codes%d" % s, align_bytes=64) for s in range(2)]
+        s_scales = [sb.tile([P, E], U8, name="s_scales%d" % s, align_bytes=64) for s in range(2)]
+        sq = [sb.tile([P, GROUPS[g][2], mc, 4], F32, name="sq%d" % i, align_bytes=64) for i, (g, m0, mc) in enumerate(PIECES)]
+        fq = [sb.tile([P, t, P, 4], BF16, name="fq%d" % g, align_bytes=64) for g, (s, n0, t) in enumerate(GROUPS)]
+        codes = [sb.tile([P, t * P], U32, name="codes%d" % g, align_bytes=64) for g, (s, n0, t) in enumerate(GROUPS)]
+        scales = [sb.tile([P, t * P], U8, name="scales%d" % g, align_bytes=64) for g, (s, n0, t) in enumerate(GROUPS)]
+        res = [sb.tile([P, 2, t, E], F32, name="res%d" % g, align_bytes=64) for g, (s, n0, t) in enumerate(GROUPS)]
+        rec = [[sb.tile([P, t], F32, name="rec%d_%d" % (g, c)) for c in range(2)] for g, (s, n0, t) in enumerate(GROUPS)]
+        banks = [[ps.tile([P, 4, E], F32, name="bank%d_%d" % (b, c)) for c in range(2)] for b in range(4)]
+        place = [(0,0),(1,0),(2,0),(3,0),(0,2)]
+        acc = [[banks[place[g][0]][c][:, place[g][1] : place[g][1] + t, :] for c in range(2)] for g, (s, n0, t) in enumerate(GROUPS)]
+
+        def load_q(i, eng):
+            s, n0, w = LOADS[i]
+            eng.dma_start(out=raw[i][:], in_=q_rows[P * s : P * s + P, :, n0 : n0 + w])
+
+        def load_s(s, eng):
+            eng.dma_start(out=s_raw[s][:], in_=s_rows[P * s : P * s + P, :, :])
+
+        def square(i):
+            g, m0, mc = PIECES[i]
+            s, n0, t = GROUPS[g]
+            first = n0 + m0 * t
+            k = [x for x, (ls, l0, lw) in enumerate(LOADS) if ls == s and l0 <= first < l0 + lw][0]
+            src = raw[k][:, :, first - LOADS[k][1] : first - LOADS[k][1] + mc * t]
+            if t == 1:
+                nc.scalar.activation(
+                    out=sq[i][:, 0, :, :].rearrange("p (c i) j -> p c j i", i=2),
+                    in_=src.rearrange("p j (c i) -> p c j i", i=2),
+                    func=ACT.Square,
+                )
+            else:
+                nc.scalar.activation(
+                    out=sq[i][:].rearrange("p r m j -> p m j r"),
+                    in_=src.rearrange("p j (m r) -> p m j r", r=t),
+                    func=ACT.Square,
+                )
+
+        def weigh(i):
+            g, m0, mc = PIECES[i]
+            t = GROUPS[g][2]
+            nc.vector.scalar_tensor_tensor(
+                out=fq[g][:, :, m0 : m0 + mc, :].rearrange("p r m j -> p r (m j)"),
+                in0=sq[i][:].rearrange("p r m j -> p r (m j)"),
+                scalar=0.125,
+                in1=wide[:, 0 : mc * 4].unsqueeze(1).to_broadcast([P, t, mc * 4]),
+                op0=ALU.add,
+                op1=ALU.mult,
+            )
+
+        def s_copy(s, on_scalar):
+            dst = s_bf[s][:].rearrange("p (c i) j -> p c j i", i=4)
+            src = s_raw[s][:].rearrange("p j (c i) -> p c j i", i=4)
+            if on_scalar:
+                nc.scalar.activation(out=dst, in_=src, func=ACT.Copy)
+            else:
+                nc.vector.tensor_copy(out=dst, in_=src)
+
+        def s_quant(s):
+            nc.vector.quantize_mx(out=s_codes[s][:].bitcast(FP8X4), scales=s_scales[s][:], in_=s_bf[s][:].rearrange("p e j -> p (e j)"))
+
+        def quant(g):
+            nc.vector.quantize_mx(out=codes[g][:].bitcast(FP8X4), scales=scales[g][:], in_=fq[g][:].rearrange("p r m j -> p (r m j)"))
+
+        def multiply(g):
+            s, n0, t = GROUPS[g]
+            for c in range(2):
+                rows = slice(64 * c, 64 * c + 64)
+                for r in range(t):
+                    cols = slice(P * r, P * r + P)
+                    nc.tensor.matmul_mx(
+                        out=acc[g][c][:, r, :],
+                        lhsT=codes[g][rows, cols].bitcast(FP8X4),
+                        lhsT_scale=scales[g][rows, cols],
+                        rhs=s_codes[s][rows, :].bitcast(FP8X4),
+                        rhs_scale=s_scales[s][rows, :],
+                        start=True,
+                        stop=True,
+                    )
+
+        def recip(g, c):
+            nc.vector.reciprocal(out=rec[g][c][:], in_=acc[g][c][:, :, E - 1])
+
+        def scale_scalar(g, c):
+            for r in range(GROUPS[g][2]):
+                nc.scalar.activation(out=res[g][:, c, r, :], in_=acc[g][c][:, r, :], func=ACT.Copy, scale=rec[g][c][:, r : r + 1])
+
+        def scale_vector(g, c):
+            t = GROUPS[g][2]
+            if t == 1:
+                nc.vector.tensor_scalar(out=res[g][:, c, 0, :], in0=acc[g][c][:, 0, :], scalar1=rec[g][c][:, 0:1], scalar2=None, op0=ALU.mult)
+            else:
+                nc.vector.tensor_tensor(out=res[g][:, c, :, :], in0=acc[g][c], in1=rec[g][c][:].unsqueeze(2).to_broadcast([P, t, E]), op=ALU.mult)
+
+        def store(g, eng):
+            s, n0, t = GROUPS[g]
+            eng.dma_start(
+                out=out[2 * s : 2 * s + 2, n0 : n0 + t * P, :].rearrange("c (m r) e -> m c (r e)", r=t),
+                in_=res[g][:].rearrange("p c r e -> p c (r e)"),
+            )
+
+        def store_head(g, c, eng):
+            s, n0, t = GROUPS[g]
+            eng.dma_start(
+                out=out[2 * s + c, n0 : n0 + t * P, :].rearrange("(m r) e -> m (r e)", r=t),
+                in_=res[g][:, c, :, :].rearrange("p r e -> p (r e)"),
+            )
+
+        queues = {"y": nc.sync, "a": nc.scalar, "g": nc.gpsimd}
+        for step in SYNC.split() + ORDER.split():
+            op, arg = step.split(":")
+            if op == "w":
+                for c in range(2):
+                    queues[arg].dma_start(out=weight[64 * c : 64 * c + 64, :], in_=qa_rows)
+            elif op == "wide":
+                mw = max(mc for g, m0, mc in PIECES)
+                nc.vector.tensor_copy(out=wide[:].rearrange("p (m j) -> p m j", j=4), in_=weight[:].unsqueeze(1).to_broadcast([P, mw, 4]))
+            elif op == "warm":
+                nc.gpsimd.memset(warm[:], 0.0)
+                nc.scalar.activation(out=warm_out[:], in_=warm[:], func=ACT.Square)
+            elif op == "lq":
+                load_q(int(arg[1:]), queues[arg[0]])
+            elif op == "ls":
+                load_s(int(arg[1:]), queues[arg[0]])
+            elif op == "sq":
+                square(int(arg))
+            elif op == "W":
+                weigh(int(arg))
+            elif op == "scv":
+                s_copy(int(arg), False)
+            elif op == "scs":
+                s_copy(int(arg), True)
+            elif op == "sQ":
+                s_quant(int(arg))
+            elif op == "Q":
+                quant(int(arg))
+            elif op == "M":
+                multiply(int(arg))
+            elif op == "R":
+                recip(int(arg[0]), int(arg[1]))
+            elif op == "es":
+                scale_scalar(int(arg[0]), int(arg[1]))
+            elif op == "ev":
+                scale_vector(int(arg[0]), int(arg[1]))
+            elif op == "st":
+                store(int(arg[1:]), queues[arg[0]])
+            else:
+                store_head(int(arg[1]), int(arg[2]), queues[arg[0]])

@@ -16,9 +16,9 @@ FLOPS = 2 * H * D * N * E
 
 GROUPS = [(0,0,2),(0,256,2),(1,0,2),(1,256,1),(1,384,1)]
 PIECES = [(0,0,64),(0,64,64),(1,0,64),(1,64,64),(2,0,64),(2,64,64),(3,0,128),(4,0,128)]
-LOADS = [(0,0,128),(0,128,128),(0,256,128),(0,384,128),(1,0,128),(1,128,128),(1,256,128),(1,384,128)]
-SYNC = "lq:y0 w:a warm:0 lq:y1 lq:y2 lq:y3 ls:y0 lq:y4 lq:y5 lq:y6 ls:y1 lq:y7"
-ORDER = "wide:0 sq:0 sq:1 W:0 W:1 sq:2 sq:3 W:2 scs:0 Q:0 W:3 sQ:0 Q:1 sq:4 M:0 W:4 R:00 sq:5 W:5 sq:6 R:01 M:1 scs:1 W:6 sQ:1 R:10 Q:3 R:11 sq:7 Q:2 M:3 W:7 es:00 R:30 M:2 es:01 ev:10 es:11 Q:4 R:31 R:21 es:30 es:31 R:20 M:4 st:y0 st:y1 ev:20 R:40 es:21 st:y3 es:40 R:41 st:y2 es:41 st:y4"
+LOADS = [(0,0,256),(0,256,256),(1,0,256),(1,256,256)]
+SYNC = "lq:y0 w:a warm:0 ls:y0 lq:y1 lq:y2 lq:y3 ls:y1"
+ORDER = "wide:0 sq:0 scv:0 sq:1 W:0 W:1 sQ:0 Q:0 sq:2 M:0 W:2 sq:3 W:3 R:01 sq:4 sq:5 R:00 Q:1 es:00 sq:6 scs:1 ev:01 W:4 W:5 W:6 M:1 sQ:1 R:11 Q:3 sq:7 st:y0 es:11 Q:2 R:10 M:3 es:10 W:7 R:30 M:2 R:31 Q:4 es:31 R:20 st:y1 M:4 R:21 ev:20 R:40 es:30 es:21 R:41 ev:40 es:41 st:y3 st:y2 st:y4"
 
 
 def tile_rows_read_sq_norm_kernel(tc, q, qa, S, out):
@@ -105,10 +105,10 @@ def tile_rows_read_sq_norm_kernel(tc, q, qa, S, out):
 
         def multiply(g):
             s, n0, t = GROUPS[g]
-            for c in range(2):
-                rows = slice(64 * c, 64 * c + 64)
-                for r in range(t):
-                    cols = slice(P * r, P * r + P)
+            for r in range(t):
+                cols = slice(P * r, P * r + P)
+                for c in range(2):
+                    rows = slice(64 * c, 64 * c + 64)
                     nc.tensor.matmul_mx(
                         out=acc[g][c][:, r, :],
                         lhsT=codes[g][rows, cols].bitcast(FP8X4),

@@ -11,179 +11,242 @@ ACT = mybir.ActivationFunctionType
 ALU = mybir.AluOpType
 
 H, D, N, E = 4, 256, 512, 128
-P = 128
 FLOPS = 2 * H * D * N * E
 
-GROUPS = [(0,0,2),(0,256,2),(1,0,2),(1,256,1),(1,384,1)]
-PIECES = [(0,0,64),(0,64,64),(1,0,64),(1,64,64),(2,0,64),(2,64,64),(3,0,128),(4,0,128)]
-LOADS = [(0,0,256),(0,256,256),(1,0,256),(1,256,256)]
-SYNC = "lq:y0 w:a warm:0 ls:y0 lq:y1 lq:y2 lq:y3 ls:y1"
-ORDER = "wide:0 sq:0 scv:0 sq:1 W:0 W:1 sQ:0 Q:0 sq:2 M:0 W:2 sq:3 W:3 R:01 sq:4 sq:5 R:00 Q:1 es:00 sq:6 scs:1 ev:01 W:4 W:5 W:6 M:1 sQ:1 R:11 Q:3 sq:7 st:y0 es:11 Q:2 R:10 M:3 es:10 W:7 R:30 M:2 R:31 Q:4 es:31 R:20 st:y1 M:4 R:21 ev:20 R:40 es:30 es:21 R:41 ev:40 es:41 st:y3 st:y2 st:y4"
+P = 128
+PACK = 4
+HEAD_ROWS = D // PACK
+SIDE = P // HEAD_ROWS
+PAIRS = H // SIDE
+PHI_OFFSET = 0.125
+TILES_IN_BANK = 4
+BANKS = 4
+
+SLABS = [(s, first) for s in range(PAIRS) for first in range(0, N, P)]
+GROUPS = [(0, 0, 2), (0, 256, 2), (1, 0, 2), (1, 256, 1), (1, 384, 1)]
+GROUP_OF_SLAB = [g for g, (s, first, t) in enumerate(GROUPS) for r in range(t)]
+PSUM_PLACE = [(0, 0), (1, 0), (2, 0), (3, 0), (0, 2)]
 
 
 def tile_rows_read_sq_norm_kernel(tc, q, qa, S, out):
     nc = tc.nc
-    q_rows = q.rearrange("h (p j) n -> (h p) j n", j=4)
-    s_rows = S.rearrange("h (p j) e -> (h p) j e", j=4)
-    qa_rows = qa.rearrange("(p j) o -> p (j o)", j=4)
+    q_rows = q.rearrange("h (p j) n -> (h p) j n", j=PACK)
+    s_rows = S.rearrange("h (p j) e -> (h p) j e", j=PACK)
+    qa_rows = qa.rearrange("(p j) o -> p (j o)", j=PACK)
 
     with ExitStack() as ctx:
         sb = ctx.enter_context(tc.tile_pool(name="sb", bufs=1))
         ps = ctx.enter_context(tc.psum_pool(name="ps", bufs=1))
         ctx.enter_context(tc.manual_schedule())
 
-        weight = sb.tile([P, 4], F32, name="weight")
-        wide = sb.tile([P, 4 * max(mc for g, m0, mc in PIECES)], F32, name="wide", align_bytes=64)
-        warm = sb.tile([P, 1], F32, name="warm")
-        warm_out = sb.tile([P, 1], F32, name="warm_out")
-        raw = [sb.tile([P, 4, w], F32, name="raw%d" % i, align_bytes=64) for i, (s, n0, w) in enumerate(LOADS)]
-        s_raw = [sb.tile([P, 4, E], F32, name="s_raw%d" % s, align_bytes=64) for s in range(2)]
-        s_bf = [sb.tile([P, E, 4], BF16, name="s_bf%d" % s, align_bytes=64) for s in range(2)]
-        s_codes = [sb.tile([P, E], U32, name="s_codes%d" % s, align_bytes=64) for s in range(2)]
-        s_scales = [sb.tile([P, E], U8, name="s_scales%d" % s, align_bytes=64) for s in range(2)]
-        sq = [sb.tile([P, GROUPS[g][2], mc, 4], F32, name="sq%d" % i, align_bytes=64) for i, (g, m0, mc) in enumerate(PIECES)]
-        fq = [sb.tile([P, t, P, 4], BF16, name="fq%d" % g, align_bytes=64) for g, (s, n0, t) in enumerate(GROUPS)]
-        codes = [sb.tile([P, t * P], U32, name="codes%d" % g, align_bytes=64) for g, (s, n0, t) in enumerate(GROUPS)]
-        scales = [sb.tile([P, t * P], U8, name="scales%d" % g, align_bytes=64) for g, (s, n0, t) in enumerate(GROUPS)]
-        res = [sb.tile([P, 2, t, E], F32, name="res%d" % g, align_bytes=64) for g, (s, n0, t) in enumerate(GROUPS)]
-        rec = [[sb.tile([P, t], F32, name="rec%d_%d" % (g, c)) for c in range(2)] for g, (s, n0, t) in enumerate(GROUPS)]
-        banks = [[ps.tile([P, 4, E], F32, name="bank%d_%d" % (b, c)) for c in range(2)] for b in range(4)]
-        place = [(0,0),(1,0),(2,0),(3,0),(0,2)]
-        acc = [[banks[place[g][0]][c][:, place[g][1] : place[g][1] + t, :] for c in range(2)] for g, (s, n0, t) in enumerate(GROUPS)]
+        weights = sb.tile([P, PACK], F32, name="weights")
+        weights_wide = sb.tile([P, P * PACK], F32, name="weights_wide", align_bytes=64)
+        q_raw = [sb.tile([P, PACK, P], F32, name="q_raw%d" % i, align_bytes=64) for i in range(len(SLABS))]
+        s_raw = [sb.tile([P, PACK, E], F32, name="s_raw%d" % s, align_bytes=64) for s in range(PAIRS)]
+        s_bf16 = [sb.tile([P, E, PACK], BF16, name="s_bf16_%d" % s, align_bytes=64) for s in range(PAIRS)]
+        s_codes = [sb.tile([P, E], U32, name="s_codes%d" % s, align_bytes=64) for s in range(PAIRS)]
+        s_scales = [sb.tile([P, E], U8, name="s_scales%d" % s, align_bytes=64) for s in range(PAIRS)]
+        squares = [
+            sb.tile([P, GROUPS[g][2], P // GROUPS[g][2], PACK], F32, name="squares%d" % i, align_bytes=64)
+            for i, g in enumerate(GROUP_OF_SLAB)
+        ]
+        sizes = [t for s, first, t in GROUPS]
+        q_bf16 = [sb.tile([P, t, P, PACK], BF16, name="q_bf16_%d" % g, align_bytes=64) for g, t in enumerate(sizes)]
+        q_codes = [sb.tile([P, t * P], U32, name="q_codes%d" % g, align_bytes=64) for g, t in enumerate(sizes)]
+        q_scales = [sb.tile([P, t * P], U8, name="q_scales%d" % g, align_bytes=64) for g, t in enumerate(sizes)]
+        result = [sb.tile([P, SIDE, t, E], F32, name="result%d" % g, align_bytes=64) for g, t in enumerate(sizes)]
+        inverse = [
+            [sb.tile([P, t], F32, name="inverse%d_%d" % (g, c)) for c in range(SIDE)] for g, t in enumerate(sizes)
+        ]
+        banks = [
+            [ps.tile([P, TILES_IN_BANK, E], F32, name="bank%d_%d" % (b, c)) for c in range(SIDE)] for b in range(BANKS)
+        ]
+        sums = [
+            [banks[b][c][:, slot : slot + t, :] for c in range(SIDE)] for (b, slot), t in zip(PSUM_PLACE, sizes)
+        ]
 
-        def load_q(i, eng):
-            s, n0, w = LOADS[i]
-            eng.dma_start(out=raw[i][:], in_=q_rows[P * s : P * s + P, :, n0 : n0 + w])
+        def load_slab(i):
+            s, first = SLABS[i]
+            nc.sync.dma_start(out=q_raw[i][:], in_=q_rows[P * s : P * s + P, :, first : first + P])
 
-        def load_s(s, eng):
-            eng.dma_start(out=s_raw[s][:], in_=s_rows[P * s : P * s + P, :, :])
+        def load_state(s):
+            nc.sync.dma_start(out=s_raw[s][:], in_=s_rows[P * s : P * s + P, :, :])
 
-        def square(i):
-            g, m0, mc = PIECES[i]
-            s, n0, t = GROUPS[g]
-            first = n0 + m0 * t
-            k = [x for x, (ls, l0, lw) in enumerate(LOADS) if ls == s and l0 <= first < l0 + lw][0]
-            src = raw[k][:, :, first - LOADS[k][1] : first - LOADS[k][1] + mc * t]
-            if t == 1:
-                nc.scalar.activation(
-                    out=sq[i][:, 0, :, :].rearrange("p (c i) j -> p c j i", i=2),
-                    in_=src.rearrange("p j (c i) -> p c j i", i=2),
-                    func=ACT.Square,
+        def load_weights():
+            for c in range(SIDE):
+                nc.sync.dma_start(out=weights[HEAD_ROWS * c : HEAD_ROWS * (c + 1), :], in_=qa_rows)
+
+        def spread_weights():
+            nc.vector.tensor_copy(
+                out=weights_wide[:].rearrange("p (m j) -> p m j", j=PACK),
+                in_=weights[:].unsqueeze(1).to_broadcast([P, P, PACK]),
+            )
+
+        def square_views(i):
+            if sizes[GROUP_OF_SLAB[i]] == 2:
+                return (
+                    squares[i][:].rearrange("p r m j -> p m j r"),
+                    q_raw[i][:].rearrange("p j (m r) -> p m j r", r=2),
                 )
-            else:
-                nc.scalar.activation(
-                    out=sq[i][:].rearrange("p r m j -> p m j r"),
-                    in_=src.rearrange("p j (m r) -> p m j r", r=t),
-                    func=ACT.Square,
-                )
+            return (
+                squares[i][:, 0, :, :].rearrange("p (k a) j -> p k j a", a=2),
+                q_raw[i][:].rearrange("p j (k a) -> p k j a", a=2),
+            )
+
+        def square_on_scalar(i):
+            dst, src = square_views(i)
+            nc.scalar.activation(out=dst, in_=src, func=ACT.Square)
+
+        def square_on_vector(i):
+            dst, src = square_views(i)
+            nc.vector.tensor_tensor(out=dst, in0=src, in1=src, op=ALU.mult)
 
         def weigh(i):
-            g, m0, mc = PIECES[i]
-            t = GROUPS[g][2]
+            g = GROUP_OF_SLAB[i]
+            t = sizes[g]
+            count = P // t
+            m0 = (SLABS[i][1] - GROUPS[g][1]) // t
             nc.vector.scalar_tensor_tensor(
-                out=fq[g][:, :, m0 : m0 + mc, :].rearrange("p r m j -> p r (m j)"),
-                in0=sq[i][:].rearrange("p r m j -> p r (m j)"),
-                scalar=0.125,
-                in1=wide[:, 0 : mc * 4].unsqueeze(1).to_broadcast([P, t, mc * 4]),
+                out=q_bf16[g][:, :, m0 : m0 + count, :].rearrange("p r m j -> p r (m j)"),
+                in0=squares[i][:].rearrange("p r m j -> p r (m j)"),
+                scalar=PHI_OFFSET,
+                in1=weights_wide[:, 0 : count * PACK].unsqueeze(1).to_broadcast([P, t, count * PACK]),
                 op0=ALU.add,
                 op1=ALU.mult,
             )
 
-        def s_copy(s, on_scalar):
-            dst = s_bf[s][:].rearrange("p (c i) j -> p c j i", i=4)
-            src = s_raw[s][:].rearrange("p j (c i) -> p c j i", i=4)
-            if on_scalar:
-                nc.scalar.activation(out=dst, in_=src, func=ACT.Copy)
-            else:
-                nc.vector.tensor_copy(out=dst, in_=src)
+        def cast_state(s):
+            nc.scalar.activation(
+                out=s_bf16[s][:].rearrange("p (k a) j -> p k j a", a=4),
+                in_=s_raw[s][:].rearrange("p j (k a) -> p k j a", a=4),
+                func=ACT.Copy,
+            )
 
-        def s_quant(s):
-            nc.vector.quantize_mx(out=s_codes[s][:].bitcast(FP8X4), scales=s_scales[s][:], in_=s_bf[s][:].rearrange("p e j -> p (e j)"))
+        def quantise_state(s):
+            nc.vector.quantize_mx(
+                out=s_codes[s][:].bitcast(FP8X4),
+                scales=s_scales[s][:],
+                in_=s_bf16[s][:].rearrange("p e j -> p (e j)"),
+            )
 
-        def quant(g):
-            nc.vector.quantize_mx(out=codes[g][:].bitcast(FP8X4), scales=scales[g][:], in_=fq[g][:].rearrange("p r m j -> p (r m j)"))
+        def quantise_queries(g):
+            nc.vector.quantize_mx(
+                out=q_codes[g][:].bitcast(FP8X4),
+                scales=q_scales[g][:],
+                in_=q_bf16[g][:].rearrange("p r m j -> p (r m j)"),
+            )
 
         def multiply(g):
-            s, n0, t = GROUPS[g]
-            for r in range(t):
+            s = GROUPS[g][0]
+            for r in range(sizes[g]):
                 cols = slice(P * r, P * r + P)
-                for c in range(2):
-                    rows = slice(64 * c, 64 * c + 64)
+                for c in range(SIDE):
+                    rows = slice(HEAD_ROWS * c, HEAD_ROWS * (c + 1))
                     nc.tensor.matmul_mx(
-                        out=acc[g][c][:, r, :],
-                        lhsT=codes[g][rows, cols].bitcast(FP8X4),
-                        lhsT_scale=scales[g][rows, cols],
+                        out=sums[g][c][:, r, :],
+                        lhsT=q_codes[g][rows, cols].bitcast(FP8X4),
+                        lhsT_scale=q_scales[g][rows, cols],
                         rhs=s_codes[s][rows, :].bitcast(FP8X4),
                         rhs_scale=s_scales[s][rows, :],
                         start=True,
                         stop=True,
                     )
 
-        def recip(g, c):
-            nc.vector.reciprocal(out=rec[g][c][:], in_=acc[g][c][:, :, E - 1])
+        def invert(g, c):
+            nc.vector.reciprocal(out=inverse[g][c][:], in_=sums[g][c][:, :, E - 1])
 
-        def scale_scalar(g, c):
-            for r in range(GROUPS[g][2]):
-                nc.scalar.activation(out=res[g][:, c, r, :], in_=acc[g][c][:, r, :], func=ACT.Copy, scale=rec[g][c][:, r : r + 1])
+        def normalise_on_scalar(g, c):
+            for r in range(sizes[g]):
+                nc.scalar.activation(
+                    out=result[g][:, c, r, :], in_=sums[g][c][:, r, :], func=ACT.Copy, scale=inverse[g][c][:, r : r + 1]
+                )
 
-        def scale_vector(g, c):
-            t = GROUPS[g][2]
+        def normalise_on_vector(g, c):
+            t = sizes[g]
             if t == 1:
-                nc.vector.tensor_scalar(out=res[g][:, c, 0, :], in0=acc[g][c][:, 0, :], scalar1=rec[g][c][:, 0:1], scalar2=None, op0=ALU.mult)
+                nc.vector.tensor_scalar(
+                    out=result[g][:, c, 0, :],
+                    in0=sums[g][c][:, 0, :],
+                    scalar1=inverse[g][c][:, 0:1],
+                    scalar2=None,
+                    op0=ALU.mult,
+                )
             else:
-                nc.vector.tensor_tensor(out=res[g][:, c, :, :], in0=acc[g][c], in1=rec[g][c][:].unsqueeze(2).to_broadcast([P, t, E]), op=ALU.mult)
+                nc.vector.tensor_tensor(
+                    out=result[g][:, c, :, :],
+                    in0=sums[g][c],
+                    in1=inverse[g][c][:].unsqueeze(2).to_broadcast([P, t, E]),
+                    op=ALU.mult,
+                )
 
-        def store(g, eng):
-            s, n0, t = GROUPS[g]
-            eng.dma_start(
-                out=out[2 * s : 2 * s + 2, n0 : n0 + t * P, :].rearrange("c (m r) e -> m c (r e)", r=t),
-                in_=res[g][:].rearrange("p c r e -> p c (r e)"),
+        def store(g):
+            s, first, t = GROUPS[g]
+            nc.sync.dma_start(
+                out=out[SIDE * s : SIDE * (s + 1), first : first + t * P, :].rearrange("c (m r) e -> m c (r e)", r=t),
+                in_=result[g][:].rearrange("p c r e -> p c (r e)"),
             )
 
-        def store_head(g, c, eng):
-            s, n0, t = GROUPS[g]
-            eng.dma_start(
-                out=out[2 * s + c, n0 : n0 + t * P, :].rearrange("(m r) e -> m (r e)", r=t),
-                in_=res[g][:, c, :, :].rearrange("p r e -> p (r e)"),
-            )
+        load_slab(0)
+        load_weights()
+        load_slab(1)
+        load_state(0)
+        for i in range(2, 7):
+            load_slab(i)
+        load_state(1)
+        load_slab(7)
 
-        queues = {"y": nc.sync, "a": nc.scalar, "g": nc.gpsimd}
-        for step in SYNC.split() + ORDER.split():
-            op, arg = step.split(":")
-            if op == "w":
-                for c in range(2):
-                    queues[arg].dma_start(out=weight[64 * c : 64 * c + 64, :], in_=qa_rows)
-            elif op == "wide":
-                mw = max(mc for g, m0, mc in PIECES)
-                nc.vector.tensor_copy(out=wide[:].rearrange("p (m j) -> p m j", j=4), in_=weight[:].unsqueeze(1).to_broadcast([P, mw, 4]))
-            elif op == "warm":
-                nc.gpsimd.memset(warm[:], 0.0)
-                nc.scalar.activation(out=warm_out[:], in_=warm[:], func=ACT.Square)
-            elif op == "lq":
-                load_q(int(arg[1:]), queues[arg[0]])
-            elif op == "ls":
-                load_s(int(arg[1:]), queues[arg[0]])
-            elif op == "sq":
-                square(int(arg))
-            elif op == "W":
-                weigh(int(arg))
-            elif op == "scv":
-                s_copy(int(arg), False)
-            elif op == "scs":
-                s_copy(int(arg), True)
-            elif op == "sQ":
-                s_quant(int(arg))
-            elif op == "Q":
-                quant(int(arg))
-            elif op == "M":
-                multiply(int(arg))
-            elif op == "R":
-                recip(int(arg[0]), int(arg[1]))
-            elif op == "es":
-                scale_scalar(int(arg[0]), int(arg[1]))
-            elif op == "ev":
-                scale_vector(int(arg[0]), int(arg[1]))
-            elif op == "st":
-                store(int(arg[1:]), queues[arg[0]])
-            else:
-                store_head(int(arg[1]), int(arg[2]), queues[arg[0]])
+        square_on_vector(0)
+        spread_weights()
+        square_on_scalar(1)
+        weigh(0)
+        weigh(1)
+        cast_state(0)
+        quantise_state(0)
+        quantise_queries(0)
+        multiply(0)
+
+        for i in range(2, 6):
+            square_on_scalar(i)
+            weigh(i)
+
+        invert(0, 1)
+        square_on_scalar(6)
+        cast_state(1)
+        normalise_on_scalar(0, 1)
+        quantise_queries(1)
+        multiply(1)
+        quantise_queries(2)
+        square_on_scalar(7)
+        invert(0, 0)
+        quantise_state(1)
+        multiply(2)
+        normalise_on_scalar(0, 0)
+        store(0)
+
+        weigh(6)
+        invert(1, 0)
+        invert(1, 1)
+        weigh(7)
+        quantise_queries(3)
+        multiply(3)
+        invert(2, 1)
+        invert(2, 0)
+        normalise_on_scalar(1, 1)
+        normalise_on_scalar(1, 0)
+        store(1)
+
+        quantise_queries(4)
+        multiply(4)
+        normalise_on_vector(2, 0)
+        normalise_on_scalar(2, 1)
+        store(2)
+
+        for g in (3, 4):
+            for c in range(SIDE):
+                invert(g, c)
+        normalise_on_scalar(3, 0)
+        normalise_on_scalar(3, 1)
+        store(3)
+        normalise_on_vector(4, 0)
+        normalise_on_scalar(4, 1)
+        store(4)

from contextlib import ExitStack

import concourse.mybir as mybir

F32 = mybir.dt.float32
BF16 = mybir.dt.bfloat16
U32 = mybir.dt.uint32
U8 = mybir.dt.uint8
FP8X4 = mybir.dt.float8_e4m3fn_x4
ACT = mybir.ActivationFunctionType
ALU = mybir.AluOpType

H, D, N, E = 4, 256, 512, 128
FLOPS = 2 * H * D * N * E

P = 128
PACK = 4
HEAD_ROWS = D // PACK
SIDE = P // HEAD_ROWS
PAIRS = H // SIDE
PHI_OFFSET = 0.125
TILES_IN_BANK = 4
BANKS = 4

SLABS = [(s, first) for s in range(PAIRS) for first in range(0, N, P)]
GROUPS = [(0, 0, 2), (0, 256, 2), (1, 0, 2), (1, 256, 1), (1, 384, 1)]
GROUP_OF_SLAB = [g for g, (s, first, t) in enumerate(GROUPS) for r in range(t)]
PSUM_PLACE = [(0, 0), (1, 0), (2, 0), (3, 0), (0, 2)]


def tile_rows_read_sq_norm_kernel(tc, q, qa, S, out):
    nc = tc.nc
    q_rows = q.rearrange("h (p j) n -> (h p) j n", j=PACK)
    s_rows = S.rearrange("h (p j) e -> (h p) j e", j=PACK)
    qa_rows = qa.rearrange("(p j) o -> p (j o)", j=PACK)

    with ExitStack() as ctx:
        sb = ctx.enter_context(tc.tile_pool(name="sb", bufs=1))
        ps = ctx.enter_context(tc.psum_pool(name="ps", bufs=1))
        ctx.enter_context(tc.manual_schedule())

        weights = sb.tile([P, PACK], F32, name="weights")
        weights_wide = sb.tile([P, P * PACK], F32, name="weights_wide", align_bytes=64)
        q_raw = [sb.tile([P, PACK, P], F32, name="q_raw%d" % i, align_bytes=64) for i in range(len(SLABS))]
        s_raw = [sb.tile([P, PACK, E], F32, name="s_raw%d" % s, align_bytes=64) for s in range(PAIRS)]
        s_bf16 = [sb.tile([P, E, PACK], BF16, name="s_bf16_%d" % s, align_bytes=64) for s in range(PAIRS)]
        s_codes = [sb.tile([P, E], U32, name="s_codes%d" % s, align_bytes=64) for s in range(PAIRS)]
        s_scales = [sb.tile([P, E], U8, name="s_scales%d" % s, align_bytes=64) for s in range(PAIRS)]
        squares = [
            sb.tile([P, GROUPS[g][2], P // GROUPS[g][2], PACK], F32, name="squares%d" % i, align_bytes=64)
            for i, g in enumerate(GROUP_OF_SLAB)
        ]
        sizes = [t for s, first, t in GROUPS]
        q_bf16 = [sb.tile([P, t, P, PACK], BF16, name="q_bf16_%d" % g, align_bytes=64) for g, t in enumerate(sizes)]
        q_codes = [sb.tile([P, t * P], U32, name="q_codes%d" % g, align_bytes=64) for g, t in enumerate(sizes)]
        q_scales = [sb.tile([P, t * P], U8, name="q_scales%d" % g, align_bytes=64) for g, t in enumerate(sizes)]
        result = [sb.tile([P, SIDE, t, E], F32, name="result%d" % g, align_bytes=64) for g, t in enumerate(sizes)]
        inverse = [
            [sb.tile([P, t], F32, name="inverse%d_%d" % (g, c)) for c in range(SIDE)] for g, t in enumerate(sizes)
        ]
        banks = [
            [ps.tile([P, TILES_IN_BANK, E], F32, name="bank%d_%d" % (b, c)) for c in range(SIDE)] for b in range(BANKS)
        ]
        sums = [
            [banks[b][c][:, slot : slot + t, :] for c in range(SIDE)] for (b, slot), t in zip(PSUM_PLACE, sizes)
        ]

        def load_slab(i):
            s, first = SLABS[i]
            nc.sync.dma_start(out=q_raw[i][:], in_=q_rows[P * s : P * s + P, :, first : first + P])

        def load_state(s):
            nc.sync.dma_start(out=s_raw[s][:], in_=s_rows[P * s : P * s + P, :, :])

        def load_weights():
            for c in range(SIDE):
                nc.sync.dma_start(out=weights[HEAD_ROWS * c : HEAD_ROWS * (c + 1), :], in_=qa_rows)

        def spread_weights():
            nc.vector.tensor_copy(
                out=weights_wide[:].rearrange("p (m j) -> p m j", j=PACK),
                in_=weights[:].unsqueeze(1).to_broadcast([P, P, PACK]),
            )

        def square_views(i):
            if sizes[GROUP_OF_SLAB[i]] == 2:
                return (
                    squares[i][:].rearrange("p r m j -> p m j r"),
                    q_raw[i][:].rearrange("p j (m r) -> p m j r", r=2),
                )
            return (
                squares[i][:, 0, :, :].rearrange("p (k a) j -> p k j a", a=2),
                q_raw[i][:].rearrange("p j (k a) -> p k j a", a=2),
            )

        def square_on_scalar(i):
            dst, src = square_views(i)
            nc.scalar.activation(out=dst, in_=src, func=ACT.Square)

        def square_on_vector(i):
            dst, src = square_views(i)
            nc.vector.tensor_tensor(out=dst, in0=src, in1=src, op=ALU.mult)

        def weigh(i):
            g = GROUP_OF_SLAB[i]
            t = sizes[g]
            count = P // t
            m0 = (SLABS[i][1] - GROUPS[g][1]) // t
            nc.vector.scalar_tensor_tensor(
                out=q_bf16[g][:, :, m0 : m0 + count, :].rearrange("p r m j -> p r (m j)"),
                in0=squares[i][:].rearrange("p r m j -> p r (m j)"),
                scalar=PHI_OFFSET,
                in1=weights_wide[:, 0 : count * PACK].unsqueeze(1).to_broadcast([P, t, count * PACK]),
                op0=ALU.add,
                op1=ALU.mult,
            )

        def cast_state(s):
            nc.scalar.activation(
                out=s_bf16[s][:].rearrange("p (k a) j -> p k j a", a=4),
                in_=s_raw[s][:].rearrange("p j (k a) -> p k j a", a=4),
                func=ACT.Copy,
            )

        def quantise_state(s):
            nc.vector.quantize_mx(
                out=s_codes[s][:].bitcast(FP8X4),
                scales=s_scales[s][:],
                in_=s_bf16[s][:].rearrange("p e j -> p (e j)"),
            )

        def quantise_queries(g):
            nc.vector.quantize_mx(
                out=q_codes[g][:].bitcast(FP8X4),
                scales=q_scales[g][:],
                in_=q_bf16[g][:].rearrange("p r m j -> p (r m j)"),
            )

        def multiply(g):
            s = GROUPS[g][0]
            for r in range(sizes[g]):
                cols = slice(P * r, P * r + P)
                for c in range(SIDE):
                    rows = slice(HEAD_ROWS * c, HEAD_ROWS * (c + 1))
                    nc.tensor.matmul_mx(
                        out=sums[g][c][:, r, :],
                        lhsT=q_codes[g][rows, cols].bitcast(FP8X4),
                        lhsT_scale=q_scales[g][rows, cols],
                        rhs=s_codes[s][rows, :].bitcast(FP8X4),
                        rhs_scale=s_scales[s][rows, :],
                        start=True,
                        stop=True,
                    )

        def invert(g, c):
            nc.vector.reciprocal(out=inverse[g][c][:], in_=sums[g][c][:, :, E - 1])

        def normalise_on_scalar(g, c):
            for r in range(sizes[g]):
                nc.scalar.activation(
                    out=result[g][:, c, r, :], in_=sums[g][c][:, r, :], func=ACT.Copy, scale=inverse[g][c][:, r : r + 1]
                )

        def normalise_on_vector(g, c):
            t = sizes[g]
            if t == 1:
                nc.vector.tensor_scalar(
                    out=result[g][:, c, 0, :],
                    in0=sums[g][c][:, 0, :],
                    scalar1=inverse[g][c][:, 0:1],
                    scalar2=None,
                    op0=ALU.mult,
                )
            else:
                nc.vector.tensor_tensor(
                    out=result[g][:, c, :, :],
                    in0=sums[g][c],
                    in1=inverse[g][c][:].unsqueeze(2).to_broadcast([P, t, E]),
                    op=ALU.mult,
                )

        def store(g):
            s, first, t = GROUPS[g]
            nc.sync.dma_start(
                out=out[SIDE * s : SIDE * (s + 1), first : first + t * P, :].rearrange("c (m r) e -> m c (r e)", r=t),
                in_=result[g][:].rearrange("p c r e -> p c (r e)"),
            )

        load_slab(0)
        load_weights()
        load_slab(1)
        load_state(0)
        for i in range(2, 7):
            load_slab(i)
        load_state(1)
        load_slab(7)

        square_on_vector(0)
        spread_weights()
        square_on_scalar(1)
        weigh(0)
        weigh(1)
        cast_state(0)
        quantise_state(0)
        quantise_queries(0)
        multiply(0)

        for i in range(2, 6):
            square_on_scalar(i)
            weigh(i)

        invert(0, 1)
        square_on_scalar(6)
        cast_state(1)
        normalise_on_scalar(0, 1)
        quantise_queries(1)
        multiply(1)
        quantise_queries(2)
        square_on_scalar(7)
        invert(0, 0)
        quantise_state(1)
        multiply(2)
        normalise_on_scalar(0, 0)
        store(0)

        weigh(6)
        invert(1, 0)
        invert(1, 1)
        weigh(7)
        quantise_queries(3)
        multiply(3)
        invert(2, 1)
        invert(2, 0)
        normalise_on_scalar(1, 1)
        normalise_on_scalar(1, 0)
        store(1)

        quantise_queries(4)
        multiply(4)
        normalise_on_vector(2, 0)
        normalise_on_scalar(2, 1)
        store(2)

        for g in (3, 4):
            for c in range(SIDE):
                invert(g, c)
        normalise_on_scalar(3, 0)
        normalise_on_scalar(3, 1)
        store(3)
        normalise_on_vector(4, 0)
        normalise_on_scalar(4, 1)
        store(4)
